import numpy as np
import ml_dtypes


def mxq(x, axis, fmt="e4m3"):
    dtype, down = {"e4m3": (ml_dtypes.float8_e4m3fn, 7), "e5m2": (ml_dtypes.float8_e5m2, 14)}[fmt]
    v = np.moveaxis(np.asarray(x, np.float32).astype(ml_dtypes.bfloat16).astype(np.float64), axis, -1)
    blocks = v.reshape(v.shape[:-1] + (-1, 32))
    amax = np.abs(blocks).max(-1, keepdims=True)
    byte = np.maximum(np.where(amax > 0, np.frexp(amax)[1] - 1 + 127, 0) - down, 1)
    scale = np.exp2(byte - 127.0)
    codes = (blocks / scale).astype(np.float32).astype(dtype).astype(np.float64)
    return np.moveaxis((codes * scale).reshape(v.shape), -1, axis)


WIDE = False


def mx_kscale(k):
    if not WIDE:
        return np.ones(k)
    levels = np.array([30, -30])
    if k % 512:
        return np.exp2(np.random.permutation(np.resize(levels, k // 32))).repeat(32)
    a = np.empty((k // 512, 16))
    for p in range(k // 512):
        a[p, :8] = np.random.permutation(np.resize(levels, 8))
        for g in range(8):
            far = levels[np.abs(levels - a[p, g]) >= 10]
            a[p, g + 8] = far[np.random.randint(len(far))]
    return np.exp2(a.ravel()).repeat(32)


def f64(x):
    return np.asarray(x).astype(np.float64)


def striped(idx):
    return np.tile(np.asarray(idx).reshape(-1, 16).T, (8, 1)).astype(np.uint16)


def unstriped(offs):
    return offs[:16].T.reshape(-1).astype(np.int64)


E2M1 = np.array([0.0, 0.5, 1.0, 1.5, 2.0, 3.0, 4.0, 6.0, -0.0, -0.5, -1.0, -1.5, -2.0, -3.0, -4.0, -6.0])


def pack_weight(w, fmt):
    k, n = w.shape
    w = f64(np.asarray(w, np.float32).astype(ml_dtypes.bfloat16)).reshape(k // 32, 32, n)
    amax = np.abs(w).max(1)
    if fmt in ("e4m3", "e5m2"):
        byte = np.frexp(amax)[1] - 1 + 127 - (7 if fmt == "e4m3" else 14)
    else:
        mant, ex = np.frexp(amax / 6.0)
        byte = np.where(mant > 0.5, ex, ex - 1) + 127
    byte = np.clip(np.where(amax > 0, byte, 1), 1, 254)
    scaled = (w * np.exp2(127.0 - byte)[:, None, :]).reshape(k, n).astype(np.float32)
    by_word = np.ascontiguousarray(scaled.reshape(k // 512, 128, 4, n).transpose(0, 1, 3, 2))
    if fmt in ("e4m3", "e5m2"):
        words = by_word.astype(ml_dtypes.float8_e4m3fn if fmt == "e4m3" else ml_dtypes.float8_e5m2).view(np.uint8)
    else:
        c = by_word.astype(ml_dtypes.float4_e2m1fn).view(np.uint8) & 0xF
        words = (c[..., 0::2] | (c[..., 1::2] << 4)).reshape(k // 512, 128, 2 * n)
    return np.ascontiguousarray(words), np.ascontiguousarray(byte.astype(np.uint8).reshape(k // 512, 16, n))


def unpack_weight(words, scales, fmt):
    g, _, n = scales.shape
    words = np.ascontiguousarray(words).reshape(g, 128, n, -1)
    if fmt in ("e4m3", "e5m2"):
        vals = words.view(ml_dtypes.float8_e4m3fn if fmt == "e4m3" else ml_dtypes.float8_e5m2).astype(np.float64)
    else:
        nib = np.empty((g, 128, n, 4), np.uint8)
        nib[..., 0::2] = words & 0xF
        nib[..., 1::2] = words >> 4
        vals = E2M1[nib]
    vals = vals * np.repeat(np.exp2(scales.astype(np.float64) - 127.0), 8, axis=1)[..., None]
    return vals.transpose(0, 1, 3, 2).reshape(g * 512, n)


K, F, T, Z, J, R, V, O, N = 512, 512, 1024, 1024, 256, 512, 1024, 128, 256


def setup_inputs():
    n = np.random.standard_normal
    idx = np.random.permutation(T)[:J]
    idx2 = np.random.permutation(Z)[:J]
    idx3 = np.random.permutation(V)[:O]
    idx4 = np.random.permutation(J)[:O]
    idx5 = np.random.permutation(T)[:O]
    fk = mx_kscale(K)
    fr = mx_kscale(R)
    ff = mx_kscale(F)
    xtp = pack_weight(n((K, T)) / fk[:, None], "e4m3")
    wp = pack_weight(n((K, R)) * 1 / np.sqrt(K) * fk[:, None] * fr, "e2m1")
    xop = pack_weight(n((F, Z)) / ff[:, None], "e2m1")
    w0p = pack_weight(n((F, R)) * 1 / np.sqrt(F) * ff[:, None] * fr, "e5m2")
    wbp = pack_weight(n((R, N)) * 1 / np.sqrt(R) / fr[:, None], "e5m2")
    wsp = pack_weight(n((K, N)) * 1 / np.sqrt(K) * fk[:, None], "e5m2")
    return {
        "xt_words": xtp[0],
        "xt_scales": xtp[1],
        "w_words": wp[0],
        "w_scales": wp[1],
        "xo_words": xop[0],
        "xo_scales": xop[1],
        "w0_words": w0p[0],
        "w0_scales": w0p[1],
        "tb": (np.random.randint(-9, 10, (R, V)).astype(np.float64)).astype(np.float32),
        "st": (np.random.uniform(0.12, 0.3, (R, 1)) * fr[:, None]).astype(np.float32),
        "sa": (np.random.uniform(0.5, 1.6, (R, 1))).astype(np.float32),
        "wb_words": wbp[0],
        "wb_scales": wbp[1],
        "ws_words": wsp[0],
        "ws_scales": wsp[1],
        "offs": striped(idx),
        "offs2": striped(idx2),
        "offs3": striped(idx3),
        "offs4": striped(idx4),
        "offs5": striped(idx5),
    }


def reference(xt_words, xt_scales, w_words, w_scales, xo_words, xo_scales, w0_words, w0_scales, tb, st, sa, wb_words, wb_scales, ws_words, ws_scales, offs, offs2, offs3, offs4, offs5):
    idx = unstriped(offs)
    idx2 = unstriped(offs2)
    idx3 = unstriped(offs3)
    idx4 = unstriped(offs4)
    idx5 = unstriped(offs5)
    xtu = unpack_weight(xt_words, xt_scales, "e4m3")
    wu = unpack_weight(w_words, w_scales, "e2m1")
    xou = unpack_weight(xo_words, xo_scales, "e2m1")
    w0u = unpack_weight(w0_words, w0_scales, "e5m2")
    wbu = unpack_weight(wb_words, wb_scales, "e5m2")
    wsu = unpack_weight(ws_words, ws_scales, "e5m2")
    xtidxg = xtu[:, idx]
    xoidx2g = xou[:, idx2]
    a = wu.T @ xtidxg + w0u.T @ xoidx2g
    hid = np.abs(f64(tb)[:, idx3] * f64(st) - a[:, idx4] * f64(sa))
    hidq = mxq(hid, 0, "e4m3")
    xtidx5g = xtu[:, idx5]
    y = wbu.T @ hidq + wsu.T @ xtidx5g
    return y

@@ -1,0 +1,191 @@
+from contextlib import ExitStack
+
+import concourse.mybir as mybir
+
+K, F, T, Z, J, R, V, O, N = 512, 512, 1024, 1024, 256, 512, 1024, 128, 256
+FLOPS = 2 * (K * R * J + F * R * J + R * N * O + K * N * O)
+
+F32 = mybir.dt.float32
+BF16 = mybir.dt.bfloat16
+I32 = mybir.dt.int32
+U32 = mybir.dt.uint32
+U16 = mybir.dt.uint16
+U8 = mybir.dt.uint8
+E4M3 = mybir.dt.float8_e4m3fn_x4
+E5M2 = mybir.dt.float8_e5m2_x4
+E2M1 = mybir.dt.float4_e2m1fn_x4
+ACT = mybir.ActivationFunctionType
+ALU = mybir.AluOpType
+
+P = 128
+PACK = 4
+QUADS = 4
+
+
+def tile_list_tableread_bank_further_plain_kernel(
+    tc, xt_words, xt_scales, w_words, w_scales, xo_words, xo_scales, w0_words, w0_scales, tb, st, sa,
+    wb_words, wb_scales, ws_words, ws_scales, offs, offs2, offs3, offs4, offs5, out,
+):
+    nc = tc.nc
+    with ExitStack() as ctx:
+        sb = ctx.enter_context(tc.tile_pool(name="sb", bufs=1))
+        ps = ctx.enter_context(tc.psum_pool(name="ps", bufs=1))
+
+        def tile(name, shape, dtype):
+            return sb.tile(shape, dtype, name=name, align_bytes=64)
+
+        l1 = tile("l1", [P, J // 16], U16)
+        l2 = tile("l2", [P, J // 16], U16)
+        l3 = tile("l3", [P, O // 16], U16)
+        l4 = tile("l4", [P, O // 16], U16)
+        l5 = tile("l5", [P, O // 16], U16)
+        xt_w = tile("xt_w", [P, T], U32)
+        xt_s = tile("xt_s", [P, T], U8)
+        xo_w = tile("xo_w", [P, Z], U16)
+        xo_s = tile("xo_s", [P, Z], U8)
+        w_w = tile("w_w", [P, R], U16)
+        w0_w = tile("w0_w", [P, R], U32)
+        wb_w = tile("wb_w", [P, N], U32)
+        ws_w = tile("ws_w", [P, N], U32)
+        width = 2 * R
+        stage = tile("stage", [PACK, QUADS, width // 4], I32)
+        plane = tile("plane", [P, width], U8)
+        late_s = tile("late_s", [P, 2 * N], U8)
+        tbt = [tile("tb%d" % t, [P, V], F32) for t in range(PACK)]
+        st4 = tile("st4", [P, PACK], F32)
+        sa4 = tile("sa4", [P, PACK], F32)
+
+        def words(x):
+            return x[0].rearrange("p n t -> p (n t)").bitcast(I32)
+
+        def load_stage(q, scales, c0, c1):
+            q.dma_start(stage[:, :, c0 // 4 : c1 // 4], scales[0].rearrange("(q r) c -> r q c", r=PACK).bitcast(I32))
+
+        def load_plane(q, dst, scales, quad, c0=0):
+            q.dma_start(dst[32 * quad : 32 * quad + 4, c0 : c0 + scales.shape[2]].bitcast(I32), scales[0, 4 * quad : 4 * quad + 4, :].bitcast(I32))
+
+        nc.vector.memset(xt_s[:].bitcast(I32), 0)
+        nc.vector.memset(xo_s[:].bitcast(I32), 0)
+        nc.vector.memset(plane[:].bitcast(I32), 0)
+        nc.vector.memset(late_s[:].bitcast(I32), 0)
+
+        tb_rows = tb.rearrange("(p t) v -> t p v", t=PACK)
+        nc.sync.dma_start(l1[:], offs)
+        load_stage(nc.scalar, w_scales, 0, R)
+        load_stage(nc.scalar, w0_scales, R, 2 * R)
+        nc.sync.dma_start(xt_w[:].bitcast(I32), words(xt_words))
+        load_plane(nc.scalar, xt_s, xt_scales, 0)
+        load_plane(nc.scalar, xt_s, xt_scales, 1)
+        nc.sync.dma_start(l2[:], offs2)
+        nc.sync.dma_start(xo_w[:].bitcast(I32), xo_words[0].bitcast(I32))
+        load_plane(nc.gpsimd, xo_s, xo_scales, 2)
+        load_plane(nc.gpsimd, xo_s, xo_scales, 3)
+        nc.gpsimd.dma_start(st4[:], st.rearrange("(p t) o -> p (t o)", t=PACK))
+        nc.gpsimd.dma_start(sa4[:], sa.rearrange("(p t) o -> p (t o)", t=PACK))
+        nc.sync.dma_start(w0_w[:].bitcast(I32), words(w0_words))
+        nc.sync.dma_start(w_w[:].bitcast(I32), w_words[0].bitcast(I32))
+        nc.sync.dma_start(tbt[0][:], tb_rows[0])
+        load_plane(nc.sync, xt_s, xt_scales, 2)
+        load_plane(nc.sync, xt_s, xt_scales, 3)
+        load_plane(nc.sync, xo_s, xo_scales, 0)
+        load_plane(nc.sync, xo_s, xo_scales, 1)
+        nc.sync.dma_start(l3[:], offs3)
+        nc.sync.dma_start(tbt[1][:], tb_rows[1])
+        nc.sync.dma_start(l4[:], offs4)
+        nc.sync.dma_start(tbt[2][:], tb_rows[2])
+        nc.sync.dma_start(l5[:], offs5)
+        load_plane(nc.sync, late_s, ws_scales, 0, N)
+        load_plane(nc.sync, late_s, ws_scales, 1, N)
+        load_plane(nc.sync, late_s, ws_scales, 2, N)
+        load_plane(nc.sync, late_s, ws_scales, 3, N)
+        nc.sync.dma_start(tbt[3][:], tb_rows[3])
+        nc.sync.dma_start(ws_w[:].bitcast(I32), words(ws_words))
+        load_plane(nc.sync, late_s, wb_scales, 0)
+        load_plane(nc.sync, late_s, wb_scales, 1)
+        load_plane(nc.sync, late_s, wb_scales, 2)
+        load_plane(nc.sync, late_s, wb_scales, 3)
+        nc.sync.dma_start(wb_w[:].bitcast(I32), words(wb_words))
+
+        for quad in range(QUADS):
+            nc.vector.tensor_copy(plane[32 * quad : 32 * quad + 4, :].bitcast(I32), stage[:, quad, :])
+
+        xtg_w = tile("xtg_w", [P, J], U32)
+        xtg_s = tile("xtg_s", [P, J], U8)
+        xog_w = tile("xog_w", [P, J], U16)
+        xog_s = tile("xog_s", [P, J], U8)
+        xt5_w = tile("xt5_w", [P, O], U32)
+        xt5_s = tile("xt5_s", [P, O], U8)
+        dealt_s = tile("dealt_s", [P, 2 * R], U8)
+        w_d = tile("w_d", [P, R], U16)
+        w0_d = tile("w0_d", [P, R], U32)
+
+        nc.vector.tensor_copy(xtg_w[:], xt_w[:].indirect(l1[:]))
+        nc.vector.tensor_copy(
+            dealt_s[:].rearrange("p (g t c i) -> p g c t i", g=2, t=PACK, i=16),
+            plane[:, 0 : 2 * R].rearrange("p (g c i t) -> p g c t i", g=2, t=PACK, i=16),
+        )
+        nc.vector.tensor_copy(xog_w[:], xo_w[:].indirect(l2[:]))
+        nc.vector.tensor_copy(xtg_s[:], xt_s[:].indirect(l1[:]))
+        nc.vector.tensor_copy(xog_s[:], xo_s[:].indirect(l2[:]))
+        nc.scalar.copy(
+            w_d[:].rearrange("p (t c i) -> p c t i", t=PACK, i=8),
+            w_w[:].rearrange("p (c i t) -> p c t i", t=PACK, i=8),
+        )
+        nc.scalar.copy(
+            w0_d[:].rearrange("p (t c i) -> p c t i", t=PACK, i=4),
+            w0_w[:].rearrange("p (c i t) -> p c t i", t=PACK, i=4),
+        )
+
+        a_ps = [ps.tile([P, J], F32, name="a_ps%d" % t) for t in range(PACK)]
+        for t in range(PACK):
+            cols = slice(P * t, P * (t + 1))
+            nc.tensor.matmul_mx(
+                out=a_ps[t][:], lhsT=w_d[:, cols].bitcast(E2M1), lhsT_scale=dealt_s[:, cols],
+                rhs=xtg_w[:].bitcast(E4M3), rhs_scale=xtg_s[:], start=True, stop=False,
+            )
+        for t in range(PACK):
+            cols = slice(P * t, P * (t + 1))
+            nc.tensor.matmul_mx(
+                out=a_ps[t][:], lhsT=w0_d[:, cols].bitcast(E5M2), lhsT_scale=dealt_s[:, R + P * t : R + P * (t + 1)],
+                rhs=xog_w[:].bitcast(E2M1), rhs_scale=xog_s[:], start=False, stop=True,
+            )
+
+        nc.vector.tensor_copy(xt5_w[:], xt_w[:].indirect(l5[:]))
+        nc.vector.tensor_copy(xt5_s[:], xt_s[:].indirect(l5[:]))
+        y_ps = [ps.tile([P, O], F32, name="y_ps%d" % h) for h in range(N // P)]
+        for h in range(N // P):
+            nc.tensor.matmul_mx(
+                out=y_ps[h][:], lhsT=ws_w[:, P * h : P * (h + 1)].bitcast(E5M2),
+                lhsT_scale=late_s[:, N + P * h : N + P * (h + 1)],
+                rhs=xt5_w[:].bitcast(E4M3), rhs_scale=xt5_s[:], start=True, stop=False,
+            )
+
+        a_sb = [tile("a_sb%d" % t, [P, J], F32) for t in range(PACK)]
+        level = [tile("level%d" % t, [P, O], F32) for t in range(PACK)]
+        held = [tile("held%d" % t, [P, O], F32) for t in range(PACK)]
+        diff = tile("diff", [P, PACK, O], F32)
+        nc.scalar.activation(out=level[0][:], in_=tbt[0][:].indirect(l3[:]), func=ACT.Copy, scale=st4[:, 0:1])
+        for t in range(PACK):
+            nc.vector.tensor_copy(a_sb[t][:], a_ps[t][:])
+            nc.scalar.activation(out=held[t][:], in_=a_sb[t][:].indirect(l4[:]), func=ACT.Copy, scale=sa4[:, t : t + 1])
+        for t in range(1, PACK):
+            nc.scalar.activation(out=level[t][:], in_=tbt[t][:].indirect(l3[:]), func=ACT.Copy, scale=st4[:, t : t + 1])
+        for t in range(PACK):
+            nc.vector.tensor_tensor(diff[:, t, :], level[t][:], held[t][:], ALU.subtract)
+
+        hid = tile("hid", [P, O * PACK], BF16)
+        hq_w = tile("hq_w", [P, O], U32)
+        hq_s = tile("hq_s", [P, O], U8)
+        nc.scalar.activation(out=hid[:].rearrange("p (o t) -> p o t", t=PACK), in_=diff[:].rearrange("p t o -> p o t"), func=ACT.Abs)
+        nc.vector.quantize_mx(out=hq_w[:].bitcast(E4M3), scales=hq_s[:], in_=hid[:])
+
+        y_sb = tile("y_sb", [P, N // P, O], F32)
+        for h in range(N // P):
+            nc.tensor.matmul_mx(
+                out=y_ps[h][:], lhsT=wb_w[:, P * h : P * (h + 1)].bitcast(E5M2),
+                lhsT_scale=late_s[:, P * h : P * (h + 1)],
+                rhs=hq_w[:].bitcast(E4M3), rhs_scale=hq_s[:], start=False, stop=True,
+            )
+        nc.vector.tensor_copy(y_sb[:, 0, :], y_ps[0][:])
+        nc.scalar.copy(y_sb[:, 1, :], y_ps[1][:])
+        nc.sync.dma_start(out.rearrange("(h p) o -> p h o", p=P), y_sb[:])

@@ -31,8 +31,8 @@ def tile_list_tableread_bank_further_plain_kernel(
         sb = ctx.enter_context(tc.tile_pool(name="sb", bufs=1))
         ps = ctx.enter_context(tc.psum_pool(name="ps", bufs=1))
 
-        def tile(name, shape, dtype):
-            return sb.tile(shape, dtype, name=name, align_bytes=64)
+        def tile(name, shape, dtype, tag=None):
+            return sb.tile(shape, dtype, name=name, tag=tag or name, align_bytes=64)
 
         l1 = tile("l1", [P, J // 16], U16)
         l2 = tile("l2", [P, J // 16], U16)
@@ -47,10 +47,10 @@ def tile_list_tableread_bank_further_plain_kernel(
         w0_w = tile("w0_w", [P, R], U32)
         wb_w = tile("wb_w", [P, N], U32)
         ws_w = tile("ws_w", [P, N], U32)
-        width = 2 * R
+        width = 2 * R + 2 * N
         stage = tile("stage", [PACK, QUADS, width // 4], I32)
+        stage_xo = tile("stage_xo", [PACK, QUADS, T // 4], I32)
         plane = tile("plane", [P, width], U8)
-        late_s = tile("late_s", [P, 2 * N], U8)
         tbt = [tile("tb%d" % t, [P, V], F32) for t in range(PACK)]
         st4 = tile("st4", [P, PACK], F32)
         sa4 = tile("sa4", [P, PACK], F32)
@@ -61,129 +61,136 @@ def tile_list_tableread_bank_further_plain_kernel(
         def load_stage(q, scales, c0, c1):
             q.dma_start(stage[:, :, c0 // 4 : c1 // 4], scales[0].rearrange("(q r) c -> r q c", r=PACK).bitcast(I32))
 
-        def load_plane(q, dst, scales, quad, c0=0):
-            q.dma_start(dst[32 * quad : 32 * quad + 4, c0 : c0 + scales.shape[2]].bitcast(I32), scales[0, 4 * quad : 4 * quad + 4, :].bitcast(I32))
+        def load_plane(q, dst, scales, quad):
+            q.dma_start(dst[32 * quad : 32 * quad + 4, :].bitcast(I32), scales[0, 4 * quad : 4 * quad + 4, :].bitcast(I32))
 
         nc.vector.memset(xt_s[:].bitcast(I32), 0)
-        nc.vector.memset(xo_s[:].bitcast(I32), 0)
         nc.vector.memset(plane[:].bitcast(I32), 0)
-        nc.vector.memset(late_s[:].bitcast(I32), 0)
+        nc.vector.memset(xo_s[:].bitcast(I32), 0)
 
         tb_rows = tb.rearrange("(p t) v -> t p v", t=PACK)
-        nc.sync.dma_start(l1[:], offs)
-        load_stage(nc.scalar, w_scales, 0, R)
+        nc.sync.dma_start(stage_xo[:], xo_scales[0].rearrange("(q r) c -> r q c", r=PACK).bitcast(I32))
         load_stage(nc.scalar, w0_scales, R, 2 * R)
-        nc.sync.dma_start(xt_w[:].bitcast(I32), words(xt_words))
-        load_plane(nc.scalar, xt_s, xt_scales, 0)
-        load_plane(nc.scalar, xt_s, xt_scales, 1)
-        nc.sync.dma_start(l2[:], offs2)
+        load_stage(nc.sync, ws_scales, 2 * R + N, width)
+        load_stage(nc.scalar, w_scales, 0, R)
         nc.sync.dma_start(xo_w[:].bitcast(I32), xo_words[0].bitcast(I32))
-        load_plane(nc.gpsimd, xo_s, xo_scales, 2)
-        load_plane(nc.gpsimd, xo_s, xo_scales, 3)
+        load_stage(nc.scalar, wb_scales, 2 * R, 2 * R + N)
         nc.gpsimd.dma_start(st4[:], st.rearrange("(p t) o -> p (t o)", t=PACK))
-        nc.gpsimd.dma_start(sa4[:], sa.rearrange("(p t) o -> p (t o)", t=PACK))
+        nc.sync.dma_start(l2[:], offs2)
+        nc.sync.dma_start(xt_w[:].bitcast(I32), words(xt_words))
         nc.sync.dma_start(w0_w[:].bitcast(I32), words(w0_words))
         nc.sync.dma_start(w_w[:].bitcast(I32), w_words[0].bitcast(I32))
         nc.sync.dma_start(tbt[0][:], tb_rows[0])
+        nc.sync.dma_start(l1[:], offs)
+        load_plane(nc.sync, xt_s, xt_scales, 0)
+        load_plane(nc.sync, xt_s, xt_scales, 1)
         load_plane(nc.sync, xt_s, xt_scales, 2)
         load_plane(nc.sync, xt_s, xt_scales, 3)
-        load_plane(nc.sync, xo_s, xo_scales, 0)
-        load_plane(nc.sync, xo_s, xo_scales, 1)
-        nc.sync.dma_start(l3[:], offs3)
         nc.sync.dma_start(tbt[1][:], tb_rows[1])
+        nc.sync.dma_start(l3[:], offs3)
         nc.sync.dma_start(l4[:], offs4)
+        nc.sync.dma_start(sa4[:], sa.rearrange("(p t) o -> p (t o)", t=PACK))
         nc.sync.dma_start(tbt[2][:], tb_rows[2])
         nc.sync.dma_start(l5[:], offs5)
-        load_plane(nc.sync, late_s, ws_scales, 0, N)
-        load_plane(nc.sync, late_s, ws_scales, 1, N)
-        load_plane(nc.sync, late_s, ws_scales, 2, N)
-        load_plane(nc.sync, late_s, ws_scales, 3, N)
         nc.sync.dma_start(tbt[3][:], tb_rows[3])
         nc.sync.dma_start(ws_w[:].bitcast(I32), words(ws_words))
-        load_plane(nc.sync, late_s, wb_scales, 0)
-        load_plane(nc.sync, late_s, wb_scales, 1)
-        load_plane(nc.sync, late_s, wb_scales, 2)
-        load_plane(nc.sync, late_s, wb_scales, 3)
         nc.sync.dma_start(wb_w[:].bitcast(I32), words(wb_words))
 
         for quad in range(QUADS):
             nc.vector.tensor_copy(plane[32 * quad : 32 * quad + 4, :].bitcast(I32), stage[:, quad, :])
+            nc.vector.tensor_copy(xo_s[32 * quad : 32 * quad + 4, :].bitcast(I32), stage_xo[:, quad, :])
 
         xtg_w = tile("xtg_w", [P, J], U32)
         xtg_s = tile("xtg_s", [P, J], U8)
         xog_w = tile("xog_w", [P, J], U16)
         xog_s = tile("xog_s", [P, J], U8)
-        xt5_w = tile("xt5_w", [P, O], U32)
-        xt5_s = tile("xt5_s", [P, O], U8)
         dealt_s = tile("dealt_s", [P, 2 * R], U8)
         w_d = tile("w_d", [P, R], U16)
         w0_d = tile("w0_d", [P, R], U32)
 
-        nc.vector.tensor_copy(xtg_w[:], xt_w[:].indirect(l1[:]))
+        nc.vector.tensor_copy(xog_w[:], xo_w[:].indirect(l2[:]))
+        nc.vector.tensor_copy(xog_s[:], xo_s[:].indirect(l2[:]))
         nc.vector.tensor_copy(
             dealt_s[:].rearrange("p (g t c i) -> p g c t i", g=2, t=PACK, i=16),
             plane[:, 0 : 2 * R].rearrange("p (g c i t) -> p g c t i", g=2, t=PACK, i=16),
         )
-        nc.vector.tensor_copy(xog_w[:], xo_w[:].indirect(l2[:]))
+        nc.vector.tensor_copy(xtg_w[:], xt_w[:].indirect(l1[:]))
         nc.vector.tensor_copy(xtg_s[:], xt_s[:].indirect(l1[:]))
-        nc.vector.tensor_copy(xog_s[:], xo_s[:].indirect(l2[:]))
-        nc.scalar.copy(
-            w_d[:].rearrange("p (t c i) -> p c t i", t=PACK, i=8),
-            w_w[:].rearrange("p (c i t) -> p c t i", t=PACK, i=8),
-        )
         nc.scalar.copy(
             w0_d[:].rearrange("p (t c i) -> p c t i", t=PACK, i=4),
             w0_w[:].rearrange("p (c i t) -> p c t i", t=PACK, i=4),
+        )
+        nc.scalar.copy(
+            w_d[:].rearrange("p (t c i) -> p c t i", t=PACK, i=8),
+            w_w[:].rearrange("p (c i t) -> p c t i", t=PACK, i=8),
         )
 
         a_ps = [ps.tile([P, J], F32, name="a_ps%d" % t) for t in range(PACK)]
         for t in range(PACK):
             cols = slice(P * t, P * (t + 1))
             nc.tensor.matmul_mx(
-                out=a_ps[t][:], lhsT=w_d[:, cols].bitcast(E2M1), lhsT_scale=dealt_s[:, cols],
-                rhs=xtg_w[:].bitcast(E4M3), rhs_scale=xtg_s[:], start=True, stop=False,
+                out=a_ps[t][:], lhsT=w0_d[:, cols].bitcast(E5M2), lhsT_scale=dealt_s[:, R + P * t : R + P * (t + 1)],
+                rhs=xog_w[:].bitcast(E2M1), rhs_scale=xog_s[:], start=True, stop=False,
             )
         for t in range(PACK):
             cols = slice(P * t, P * (t + 1))
             nc.tensor.matmul_mx(
-                out=a_ps[t][:], lhsT=w0_d[:, cols].bitcast(E5M2), lhsT_scale=dealt_s[:, R + P * t : R + P * (t + 1)],
-                rhs=xog_w[:].bitcast(E2M1), rhs_scale=xog_s[:], start=False, stop=True,
+                out=a_ps[t][:], lhsT=w_d[:, cols].bitcast(E2M1), lhsT_scale=dealt_s[:, cols],
+                rhs=xtg_w[:].bitcast(E4M3), rhs_scale=xtg_s[:], start=False, stop=True,
             )
 
+        level = tile("level", [P, PACK, O], F32)
+        held = {}
+        diff = tile("diff", [P, PACK, O], F32)
+
+        def fetch_level(t):
+            nc.scalar.activation(out=level[:, t, :], in_=tbt[t][:].indirect(l3[:]), func=ACT.Copy, scale=st4[:, t : t + 1])
+
+        def fetch_held(t, tag):
+            a_sb = tile("a_sb%d" % t, [P, J], F32)
+            if t % 2 == 0:
+                held[t // 2] = tile("held%d" % (t // 2), [P, 2, O], F32, tag)
+            nc.vector.tensor_copy(a_sb[:], a_ps[t][:])
+            nc.scalar.activation(out=held[t // 2][:, t % 2, :], in_=a_sb[:].indirect(l4[:]), func=ACT.Copy, scale=sa4[:, t : t + 1])
+
+        fetch_level(0)
+        fetch_level(1)
+        fetch_held(0, "tb1")
+        fetch_held(1, None)
+        fetch_level(2)
+        fetch_held(2, "tb2")
+        fetch_held(3, None)
+        fetch_level(3)
+
+        xt5_w = tile("xt5_w", [P, O], U32, "xtg_w")
+        xt5_s = tile("xt5_s", [P, O], U8, "xtg_s")
         nc.vector.tensor_copy(xt5_w[:], xt_w[:].indirect(l5[:]))
         nc.vector.tensor_copy(xt5_s[:], xt_s[:].indirect(l5[:]))
         y_ps = [ps.tile([P, O], F32, name="y_ps%d" % h) for h in range(N // P)]
         for h in range(N // P):
             nc.tensor.matmul_mx(
                 out=y_ps[h][:], lhsT=ws_w[:, P * h : P * (h + 1)].bitcast(E5M2),
-                lhsT_scale=late_s[:, N + P * h : N + P * (h + 1)],
+                lhsT_scale=plane[:, 2 * R + N + P * h : 2 * R + N + P * (h + 1)],
                 rhs=xt5_w[:].bitcast(E4M3), rhs_scale=xt5_s[:], start=True, stop=False,
             )
 
-        a_sb = [tile("a_sb%d" % t, [P, J], F32) for t in range(PACK)]
-        level = [tile("level%d" % t, [P, O], F32) for t in range(PACK)]
-        held = [tile("held%d" % t, [P, O], F32) for t in range(PACK)]
-        diff = tile("diff", [P, PACK, O], F32)
-        nc.scalar.activation(out=level[0][:], in_=tbt[0][:].indirect(l3[:]), func=ACT.Copy, scale=st4[:, 0:1])
-        for t in range(PACK):
-            nc.vector.tensor_copy(a_sb[t][:], a_ps[t][:])
-            nc.scalar.activation(out=held[t][:], in_=a_sb[t][:].indirect(l4[:]), func=ACT.Copy, scale=sa4[:, t : t + 1])
-        for t in range(1, PACK):
-            nc.scalar.activation(out=level[t][:], in_=tbt[t][:].indirect(l3[:]), func=ACT.Copy, scale=st4[:, t : t + 1])
-        for t in range(PACK):
-            nc.vector.tensor_tensor(diff[:, t, :], level[t][:], held[t][:], ALU.subtract)
-
-        hid = tile("hid", [P, O * PACK], BF16)
+        hid = tile("hid", [P, O * PACK], BF16, "tb3")
         hq_w = tile("hq_w", [P, O], U32)
         hq_s = tile("hq_s", [P, O], U8)
-        nc.scalar.activation(out=hid[:].rearrange("p (o t) -> p o t", t=PACK), in_=diff[:].rearrange("p t o -> p o t"), func=ACT.Abs)
+        hid_ot = hid[:].rearrange("p (o t) -> p o t", t=PACK)
+        diff_ot = diff[:].rearrange("p t o -> p o t")
+        nc.vector.tensor_tensor(diff[:, 0:2, :], level[:, 0:2, :], held[0][:], ALU.subtract)
+        nc.scalar.activation(out=hid_ot[:, :, 0:2], in_=diff_ot[:, :, 0:2], func=ACT.Abs)
+        for t in range(2, PACK):
+            nc.vector.tensor_tensor(diff[:, t, :], level[:, t, :], held[1][:, t - 2, :], ALU.subtract)
+        nc.scalar.activation(out=hid_ot[:, :, 2:4], in_=diff_ot[:, :, 2:4], func=ACT.Abs)
         nc.vector.quantize_mx(out=hq_w[:].bitcast(E4M3), scales=hq_s[:], in_=hid[:])
 
         y_sb = tile("y_sb", [P, N // P, O], F32)
         for h in range(N // P):
             nc.tensor.matmul_mx(
                 out=y_ps[h][:], lhsT=wb_w[:, P * h : P * (h + 1)].bitcast(E5M2),
-                lhsT_scale=late_s[:, P * h : P * (h + 1)],
+                lhsT_scale=plane[:, 2 * R + P * h : 2 * R + P * (h + 1)],
                 rhs=hq_w[:].bitcast(E4M3), rhs_scale=hq_s[:], start=False, stop=True,
             )
         nc.vector.tensor_copy(y_sb[:, 0, :], y_ps[0][:])

@@ -19,7 +19,11 @@ ALU = mybir.AluOpType
 
 P = 128
 PACK = 4
-QUADS = 4
+QUAD = 32
+QUADS = P // QUAD
+HALF = P // 2
+LIST_COL = 16
+LINE = 16
 
 
 def tile_list_tableread_bank_further_plain_kernel(
@@ -34,164 +38,176 @@ def tile_list_tableread_bank_further_plain_kernel(
         def tile(name, shape, dtype, tag=None):
             return sb.tile(shape, dtype, name=name, tag=tag or name, align_bytes=64)
 
-        l1 = tile("l1", [P, J // 16], U16)
-        l2 = tile("l2", [P, J // 16], U16)
-        l3 = tile("l3", [P, O // 16], U16)
-        l4 = tile("l4", [P, O // 16], U16)
-        l5 = tile("l5", [P, O // 16], U16)
+        list1 = tile("list1", [P, J // LIST_COL], U16)
+        list2 = tile("list2", [P, J // LIST_COL], U16)
+        list3 = tile("list3", [P, O // LIST_COL], U16)
+        list4 = tile("list4", [P, O // LIST_COL], U16)
+        list5 = tile("list5", [P, O // LIST_COL], U16)
         xt_w = tile("xt_w", [P, T], U32)
-        xt_s = tile("xt_s", [P, T], U8)
+        xt_plane = tile("xt_plane", [P, T], U8)
         xo_w = tile("xo_w", [P, Z], U16)
-        xo_s = tile("xo_s", [P, Z], U8)
+        xo_plane = tile("xo_plane", [P, Z], U8)
         w_w = tile("w_w", [P, R], U16)
         w0_w = tile("w0_w", [P, R], U32)
         wb_w = tile("wb_w", [P, N], U32)
         ws_w = tile("ws_w", [P, N], U32)
-        width = 2 * R + 2 * N
-        stage = tile("stage", [PACK, QUADS, width // 4], I32)
-        stage_xo = tile("stage_xo", [PACK, QUADS, T // 4], I32)
-        plane = tile("plane", [P, width], U8)
-        tbt = [tile("tb%d" % t, [P, V], F32) for t in range(PACK)]
-        st4 = tile("st4", [P, PACK], F32)
-        sa4 = tile("sa4", [P, PACK], F32)
+        first_stage = tile("first_stage", [HALF + PACK, 2, 2 * R // 4], I32)
+        xo_stage = tile("xo_stage", [HALF + PACK, 2, Z // 4], I32)
+        last_plane = tile("last_plane", [P, 2 * N], U8)
+        first_plane = tile("first_plane", [P, 2 * R], U8)
+        tb_slices = [tile("tb%d" % t, [P, V], F32) for t in range(PACK)]
+        st_cols = tile("st_cols", [P, PACK], F32)
+        sa_cols = tile("sa_cols", [P, PACK], F32)
 
-        def words(x):
-            return x[0].rearrange("p n t -> p (n t)").bitcast(I32)
+        def load_fp8_words(dst, src):
+            nc.sync.dma_start(dst[:].bitcast(I32), src[0].rearrange("p n t -> p (n t)").bitcast(I32))
 
-        def load_stage(q, scales, c0, c1):
-            q.dma_start(stage[:, :, c0 // 4 : c1 // 4], scales[0].rearrange("(q r) c -> r q c", r=PACK).bitcast(I32))
+        def load_fp4_words(dst, src):
+            nc.sync.dma_start(dst[:].bitcast(I32), src[0].bitcast(I32))
 
-        def load_plane(q, dst, scales, quad):
-            q.dma_start(dst[32 * quad : 32 * quad + 4, :].bitcast(I32), scales[0, 4 * quad : 4 * quad + 4, :].bitcast(I32))
+        def load_stage(queue, dst, scales, half, col):
+            rows = scales[0, 2 * PACK * half : 2 * PACK * (half + 1), :].rearrange("(q i) c -> i q c", i=PACK)
+            words = slice(col // 4, (col + scales.shape[2]) // 4)
+            queue.dma_start(dst[HALF * half : HALF * half + PACK, :, words], rows.bitcast(I32))
 
-        nc.vector.memset(xt_s[:].bitcast(I32), 0)
-        nc.vector.memset(plane[:].bitcast(I32), 0)
-        nc.vector.memset(xo_s[:].bitcast(I32), 0)
+        def load_plane_rows(dst, scales, col, places):
+            for i in places:
+                rows = scales[0, i : PACK * QUADS : PACK, :]
+                nc.sync.dma_start(dst[i:P:QUAD, col : col + scales.shape[2]].bitcast(I32), rows.bitcast(I32))
 
-        tb_rows = tb.rearrange("(p t) v -> t p v", t=PACK)
-        nc.sync.dma_start(stage_xo[:], xo_scales[0].rearrange("(q r) c -> r q c", r=PACK).bitcast(I32))
-        load_stage(nc.scalar, w0_scales, R, 2 * R)
-        load_stage(nc.sync, ws_scales, 2 * R + N, width)
-        load_stage(nc.scalar, w_scales, 0, R)
-        nc.sync.dma_start(xo_w[:].bitcast(I32), xo_words[0].bitcast(I32))
-        load_stage(nc.scalar, wb_scales, 2 * R, 2 * R + N)
-        nc.gpsimd.dma_start(st4[:], st.rearrange("(p t) o -> p (t o)", t=PACK))
-        nc.sync.dma_start(l2[:], offs2)
-        nc.sync.dma_start(xt_w[:].bitcast(I32), words(xt_words))
-        nc.sync.dma_start(w0_w[:].bitcast(I32), words(w0_words))
-        nc.sync.dma_start(w_w[:].bitcast(I32), w_words[0].bitcast(I32))
-        nc.sync.dma_start(tbt[0][:], tb_rows[0])
-        nc.sync.dma_start(l1[:], offs)
-        load_plane(nc.sync, xt_s, xt_scales, 0)
-        load_plane(nc.sync, xt_s, xt_scales, 1)
-        load_plane(nc.sync, xt_s, xt_scales, 2)
-        load_plane(nc.sync, xt_s, xt_scales, 3)
-        nc.sync.dma_start(tbt[1][:], tb_rows[1])
-        nc.sync.dma_start(l3[:], offs3)
-        nc.sync.dma_start(l4[:], offs4)
-        nc.sync.dma_start(sa4[:], sa.rearrange("(p t) o -> p (t o)", t=PACK))
-        nc.sync.dma_start(tbt[2][:], tb_rows[2])
-        nc.sync.dma_start(l5[:], offs5)
-        nc.sync.dma_start(tbt[3][:], tb_rows[3])
-        nc.sync.dma_start(ws_w[:].bitcast(I32), words(ws_words))
-        nc.sync.dma_start(wb_w[:].bitcast(I32), words(wb_words))
+        def load_tb(t):
+            nc.sync.dma_start(tb_slices[t][:], tb.rearrange("(p t) v -> t p v", t=PACK)[t])
 
-        for quad in range(QUADS):
-            nc.vector.tensor_copy(plane[32 * quad : 32 * quad + 4, :].bitcast(I32), stage[:, quad, :])
-            nc.vector.tensor_copy(xo_s[32 * quad : 32 * quad + 4, :].bitcast(I32), stage_xo[:, quad, :])
+        def load_row_values(dst, src):
+            nc.sync.dma_start(dst[:], src.rearrange("(p t) o -> p (t o)", t=PACK))
 
-        xtg_w = tile("xtg_w", [P, J], U32)
-        xtg_s = tile("xtg_s", [P, J], U8)
-        xog_w = tile("xog_w", [P, J], U16)
-        xog_s = tile("xog_s", [P, J], U8)
-        dealt_s = tile("dealt_s", [P, 2 * R], U8)
-        w_d = tile("w_d", [P, R], U16)
-        w0_d = tile("w0_d", [P, R], U32)
+        for plane in (xt_plane, last_plane, first_plane, xo_plane):
+            nc.vector.memset(plane[:].bitcast(I32), 0)
 
-        nc.vector.tensor_copy(xog_w[:], xo_w[:].indirect(l2[:]))
-        nc.vector.tensor_copy(xog_s[:], xo_s[:].indirect(l2[:]))
+        load_stage(nc.sync, xo_stage, xo_scales, 0, 0)
+        load_stage(nc.scalar, first_stage, w0_scales, 1, R)
+        load_stage(nc.sync, xo_stage, xo_scales, 1, 0)
+        load_stage(nc.scalar, first_stage, w0_scales, 0, R)
+        load_stage(nc.sync, first_stage, w_scales, 0, 0)
+        load_stage(nc.scalar, first_stage, w_scales, 1, 0)
+        load_fp4_words(xo_w, xo_words)
+        load_fp8_words(xt_w, xt_words)
+        nc.sync.dma_start(list2[:], offs2)
+        load_fp8_words(w0_w, w0_words)
+        load_fp4_words(w_w, w_words)
+        nc.sync.dma_start(list1[:], offs)
+        nc.sync.dma_start(list3[:], offs3)
+        load_tb(0)
+        load_plane_rows(xt_plane, xt_scales, 0, range(PACK))
+        load_row_values(st_cols, st)
+        load_row_values(sa_cols, sa)
+        load_tb(1)
+        nc.sync.dma_start(list5[:], offs5)
+        nc.sync.dma_start(list4[:], offs4)
+        load_tb(2)
+        load_plane_rows(last_plane, ws_scales, N, range(PACK - 1))
+        load_tb(3)
+        load_fp8_words(ws_w, ws_words)
+        load_plane_rows(last_plane, ws_scales, N, range(PACK - 1, PACK))
+        load_fp8_words(wb_w, wb_words)
+        load_plane_rows(last_plane, wb_scales, 0, range(PACK))
+
+        for q in range(QUADS):
+            live = slice(QUAD * q, QUAD * q + PACK)
+            staged = slice(HALF * (q // 2), HALF * (q // 2) + PACK)
+            nc.vector.tensor_copy(first_plane[live, :].bitcast(I32), first_stage[staged, q % 2, :])
+            nc.vector.tensor_copy(xo_plane[live, :].bitcast(I32), xo_stage[staged, q % 2, :])
+
+        xt1_w = tile("xt1_w", [P, J], U32)
+        xt1_plane = tile("xt1_plane", [P, J], U8)
+        xo2_w = tile("xo2_w", [P, J], U16)
+        xo2_plane = tile("xo2_plane", [P, J], U8)
+        dealt_plane = tile("dealt_plane", [P, 2 * R], U8)
+        w_dealt = tile("w_dealt", [P, R], U16)
+        w0_dealt = tile("w0_dealt", [P, R], U32)
+
         nc.vector.tensor_copy(
-            dealt_s[:].rearrange("p (g t c i) -> p g c t i", g=2, t=PACK, i=16),
-            plane[:, 0 : 2 * R].rearrange("p (g c i t) -> p g c t i", g=2, t=PACK, i=16),
+            dealt_plane[:].rearrange("p (g t c i) -> p g c t i", g=2, t=PACK, i=LINE),
+            first_plane[:].rearrange("p (g c i t) -> p g c t i", g=2, t=PACK, i=LINE),
         )
-        nc.vector.tensor_copy(xtg_w[:], xt_w[:].indirect(l1[:]))
-        nc.vector.tensor_copy(xtg_s[:], xt_s[:].indirect(l1[:]))
-        nc.scalar.copy(
-            w0_d[:].rearrange("p (t c i) -> p c t i", t=PACK, i=4),
-            w0_w[:].rearrange("p (c i t) -> p c t i", t=PACK, i=4),
-        )
-        nc.scalar.copy(
-            w_d[:].rearrange("p (t c i) -> p c t i", t=PACK, i=8),
-            w_w[:].rearrange("p (c i t) -> p c t i", t=PACK, i=8),
-        )
+        nc.vector.tensor_copy(xo2_w[:], xo_w[:].indirect(list2[:]))
+        nc.vector.tensor_copy(xo2_plane[:], xo_plane[:].indirect(list2[:]))
+        nc.vector.tensor_copy(xt1_w[:], xt_w[:].indirect(list1[:]))
+        nc.vector.tensor_copy(xt1_plane[:], xt_plane[:].indirect(list1[:]))
+        for dealt, loaded, word_bytes in ((w0_dealt, w0_w, 4), (w_dealt, w_w, 2)):
+            nc.scalar.copy(
+                dealt[:].rearrange("p (t c i) -> p c t i", t=PACK, i=LINE // word_bytes),
+                loaded[:].rearrange("p (c i t) -> p c t i", t=PACK, i=LINE // word_bytes),
+            )
 
         a_ps = [ps.tile([P, J], F32, name="a_ps%d" % t) for t in range(PACK)]
         for t in range(PACK):
-            cols = slice(P * t, P * (t + 1))
             nc.tensor.matmul_mx(
-                out=a_ps[t][:], lhsT=w0_d[:, cols].bitcast(E5M2), lhsT_scale=dealt_s[:, R + P * t : R + P * (t + 1)],
-                rhs=xog_w[:].bitcast(E2M1), rhs_scale=xog_s[:], start=True, stop=False,
+                out=a_ps[t][:], lhsT=w0_dealt[:, P * t : P * (t + 1)].bitcast(E5M2),
+                lhsT_scale=dealt_plane[:, R + P * t : R + P * (t + 1)],
+                rhs=xo2_w[:].bitcast(E2M1), rhs_scale=xo2_plane[:], start=True, stop=False,
             )
         for t in range(PACK):
-            cols = slice(P * t, P * (t + 1))
             nc.tensor.matmul_mx(
-                out=a_ps[t][:], lhsT=w_d[:, cols].bitcast(E2M1), lhsT_scale=dealt_s[:, cols],
-                rhs=xtg_w[:].bitcast(E4M3), rhs_scale=xtg_s[:], start=False, stop=True,
+                out=a_ps[t][:], lhsT=w_dealt[:, P * t : P * (t + 1)].bitcast(E2M1),
+                lhsT_scale=dealt_plane[:, P * t : P * (t + 1)],
+                rhs=xt1_w[:].bitcast(E4M3), rhs_scale=xt1_plane[:], start=False, stop=True,
             )
 
-        level = tile("level", [P, PACK, O], F32)
-        held = {}
-        diff = tile("diff", [P, PACK, O], F32)
-
-        def fetch_level(t):
-            nc.scalar.activation(out=level[:, t, :], in_=tbt[t][:].indirect(l3[:]), func=ACT.Copy, scale=st4[:, t : t + 1])
-
-        def fetch_held(t, tag):
-            a_sb = tile("a_sb%d" % t, [P, J], F32)
-            if t % 2 == 0:
-                held[t // 2] = tile("held%d" % (t // 2), [P, 2, O], F32, tag)
-            nc.vector.tensor_copy(a_sb[:], a_ps[t][:])
-            nc.scalar.activation(out=held[t // 2][:, t % 2, :], in_=a_sb[:].indirect(l4[:]), func=ACT.Copy, scale=sa4[:, t : t + 1])
-
-        fetch_level(0)
-        fetch_level(1)
-        fetch_held(0, "tb1")
-        fetch_held(1, None)
-        fetch_level(2)
-        fetch_held(2, "tb2")
-        fetch_held(3, None)
-        fetch_level(3)
-
-        xt5_w = tile("xt5_w", [P, O], U32, "xtg_w")
-        xt5_s = tile("xt5_s", [P, O], U8, "xtg_s")
-        nc.vector.tensor_copy(xt5_w[:], xt_w[:].indirect(l5[:]))
-        nc.vector.tensor_copy(xt5_s[:], xt_s[:].indirect(l5[:]))
+        xt5_w = tile("xt5_w", [P, O], U32)
+        xt5_plane = tile("xt5_plane", [P, O], U8)
+        nc.vector.tensor_copy(xt5_w[:], xt_w[:].indirect(list5[:]))
+        nc.vector.tensor_copy(xt5_plane[:], xt_plane[:].indirect(list5[:]))
         y_ps = [ps.tile([P, O], F32, name="y_ps%d" % h) for h in range(N // P)]
         for h in range(N // P):
             nc.tensor.matmul_mx(
                 out=y_ps[h][:], lhsT=ws_w[:, P * h : P * (h + 1)].bitcast(E5M2),
-                lhsT_scale=plane[:, 2 * R + N + P * h : 2 * R + N + P * (h + 1)],
-                rhs=xt5_w[:].bitcast(E4M3), rhs_scale=xt5_s[:], start=True, stop=False,
+                lhsT_scale=last_plane[:, N + P * h : N + P * (h + 1)],
+                rhs=xt5_w[:].bitcast(E4M3), rhs_scale=xt5_plane[:], start=True, stop=False,
             )
 
-        hid = tile("hid", [P, O * PACK], BF16, "tb3")
-        hq_w = tile("hq_w", [P, O], U32)
-        hq_s = tile("hq_s", [P, O], U8)
+        level = tile("level", [P, PACK, O], F32)
+        diff = tile("diff", [P, PACK, O], F32)
+
+        def fetch_level(t):
+            nc.scalar.activation(
+                out=level[:, t, :], in_=tb_slices[t][:].indirect(list3[:]), func=ACT.Copy, scale=st_cols[:, t : t + 1]
+            )
+
+        def fetch_weighted(t, dst):
+            a_sb = tile("a_sb%d" % t, [P, J], F32)
+            nc.vector.tensor_copy(a_sb[:], a_ps[t][:])
+            nc.scalar.activation(out=dst, in_=a_sb[:].indirect(list4[:]), func=ACT.Copy, scale=sa_cols[:, t : t + 1])
+
+        fetch_level(0)
+        fetch_level(1)
+        weighted_low = tile("weighted_low", [P, 2, O], F32, "tb1")
+        weighted_high = tile("weighted_high", [P, 2, O], F32)
+        for t in range(PACK):
+            fetch_weighted(t, (weighted_low, weighted_high)[t // 2][:, t % 2, :])
+        fetch_level(2)
+        fetch_level(3)
+
+        hid = tile("hid", [P, O * PACK], BF16)
+        hid_w = tile("hid_w", [P, O], U32)
+        hid_plane = tile("hid_plane", [P, O], U8)
         hid_ot = hid[:].rearrange("p (o t) -> p o t", t=PACK)
         diff_ot = diff[:].rearrange("p t o -> p o t")
-        nc.vector.tensor_tensor(diff[:, 0:2, :], level[:, 0:2, :], held[0][:], ALU.subtract)
-        nc.scalar.activation(out=hid_ot[:, :, 0:2], in_=diff_ot[:, :, 0:2], func=ACT.Abs)
+        nc.vector.tensor_tensor(diff[:, 0:2, :], level[:, 0:2, :], weighted_low[:], ALU.subtract)
+        nc.vector.scalar_tensor_tensor(
+            hid_ot[:, :, 0:2], diff_ot[:, :, 0:2], -1.0, diff_ot[:, :, 0:2], ALU.mult, ALU.max
+        )
         for t in range(2, PACK):
-            nc.vector.tensor_tensor(diff[:, t, :], level[:, t, :], held[1][:, t - 2, :], ALU.subtract)
+            nc.vector.tensor_tensor(diff[:, t, :], level[:, t, :], weighted_high[:, t - 2, :], ALU.subtract)
         nc.scalar.activation(out=hid_ot[:, :, 2:4], in_=diff_ot[:, :, 2:4], func=ACT.Abs)
-        nc.vector.quantize_mx(out=hq_w[:].bitcast(E4M3), scales=hq_s[:], in_=hid[:])
+        nc.vector.quantize_mx(out=hid_w[:].bitcast(E4M3), scales=hid_plane[:], in_=hid[:])
 
         y_sb = tile("y_sb", [P, N // P, O], F32)
         for h in range(N // P):
             nc.tensor.matmul_mx(
                 out=y_ps[h][:], lhsT=wb_w[:, P * h : P * (h + 1)].bitcast(E5M2),
-                lhsT_scale=plane[:, 2 * R + P * h : 2 * R + P * (h + 1)],
-                rhs=hq_w[:].bitcast(E4M3), rhs_scale=hq_s[:], start=False, stop=True,
+                lhsT_scale=last_plane[:, P * h : P * (h + 1)],
+                rhs=hid_w[:].bitcast(E4M3), rhs_scale=hid_plane[:], start=False, stop=True,
             )
         nc.vector.tensor_copy(y_sb[:, 0, :], y_ps[0][:])
         nc.scalar.copy(y_sb[:, 1, :], y_ps[1][:])

from contextlib import ExitStack

import concourse.mybir as mybir

K, F, T, Z, J, R, V, O, N = 512, 512, 1024, 1024, 256, 512, 1024, 128, 256
FLOPS = 2 * (K * R * J + F * R * J + R * N * O + K * N * O)

F32 = mybir.dt.float32
BF16 = mybir.dt.bfloat16
I32 = mybir.dt.int32
U32 = mybir.dt.uint32
U16 = mybir.dt.uint16
U8 = mybir.dt.uint8
E4M3 = mybir.dt.float8_e4m3fn_x4
E5M2 = mybir.dt.float8_e5m2_x4
E2M1 = mybir.dt.float4_e2m1fn_x4
ACT = mybir.ActivationFunctionType
ALU = mybir.AluOpType

P = 128
PACK = 4
QUAD = 32
QUADS = P // QUAD
HALF = P // 2
LIST_COL = 16
LINE = 16


def tile_list_tableread_bank_further_plain_kernel(
    tc, xt_words, xt_scales, w_words, w_scales, xo_words, xo_scales, w0_words, w0_scales, tb, st, sa,
    wb_words, wb_scales, ws_words, ws_scales, offs, offs2, offs3, offs4, offs5, out,
):
    nc = tc.nc
    with ExitStack() as ctx:
        sb = ctx.enter_context(tc.tile_pool(name="sb", bufs=1))
        ps = ctx.enter_context(tc.psum_pool(name="ps", bufs=1))

        def tile(name, shape, dtype, tag=None):
            return sb.tile(shape, dtype, name=name, tag=tag or name, align_bytes=64)

        list1 = tile("list1", [P, J // LIST_COL], U16)
        list2 = tile("list2", [P, J // LIST_COL], U16)
        list3 = tile("list3", [P, O // LIST_COL], U16)
        list4 = tile("list4", [P, O // LIST_COL], U16)
        list5 = tile("list5", [P, O // LIST_COL], U16)
        xt_w = tile("xt_w", [P, T], U32)
        xt_plane = tile("xt_plane", [P, T], U8)
        xo_w = tile("xo_w", [P, Z], U16)
        xo_plane = tile("xo_plane", [P, Z], U8)
        w_w = tile("w_w", [P, R], U16)
        w0_w = tile("w0_w", [P, R], U32)
        wb_w = tile("wb_w", [P, N], U32)
        ws_w = tile("ws_w", [P, N], U32)
        first_stage = tile("first_stage", [HALF + PACK, 2, 2 * R // 4], I32)
        xo_stage = tile("xo_stage", [HALF + PACK, 2, Z // 4], I32)
        last_plane = tile("last_plane", [P, 2 * N], U8)
        first_plane = tile("first_plane", [P, 2 * R], U8)
        tb_slices = [tile("tb%d" % t, [P, V], F32) for t in range(PACK)]
        st_cols = tile("st_cols", [P, PACK], F32)
        sa_cols = tile("sa_cols", [P, PACK], F32)

        def load_fp8_words(dst, src):
            nc.sync.dma_start(dst[:].bitcast(I32), src[0].rearrange("p n t -> p (n t)").bitcast(I32))

        def load_fp4_words(dst, src):
            nc.sync.dma_start(dst[:].bitcast(I32), src[0].bitcast(I32))

        def load_stage(queue, dst, scales, half, col):
            rows = scales[0, 2 * PACK * half : 2 * PACK * (half + 1), :].rearrange("(q i) c -> i q c", i=PACK)
            words = slice(col // 4, (col + scales.shape[2]) // 4)
            queue.dma_start(dst[HALF * half : HALF * half + PACK, :, words], rows.bitcast(I32))

        def load_plane_rows(dst, scales, col, places):
            for i in places:
                rows = scales[0, i : PACK * QUADS : PACK, :]
                nc.sync.dma_start(dst[i:P:QUAD, col : col + scales.shape[2]].bitcast(I32), rows.bitcast(I32))

        def load_tb(t):
            nc.sync.dma_start(tb_slices[t][:], tb.rearrange("(p t) v -> t p v", t=PACK)[t])

        def load_row_values(dst, src):
            nc.sync.dma_start(dst[:], src.rearrange("(p t) o -> p (t o)", t=PACK))

        for plane in (xt_plane, last_plane, first_plane, xo_plane):
            nc.vector.memset(plane[:].bitcast(I32), 0)

        load_stage(nc.sync, xo_stage, xo_scales, 0, 0)
        load_stage(nc.scalar, first_stage, w0_scales, 1, R)
        load_stage(nc.sync, xo_stage, xo_scales, 1, 0)
        load_stage(nc.scalar, first_stage, w0_scales, 0, R)
        load_stage(nc.sync, first_stage, w_scales, 0, 0)
        load_stage(nc.scalar, first_stage, w_scales, 1, 0)
        load_fp4_words(xo_w, xo_words)
        load_fp8_words(xt_w, xt_words)
        nc.sync.dma_start(list2[:], offs2)
        load_fp8_words(w0_w, w0_words)
        load_fp4_words(w_w, w_words)
        nc.sync.dma_start(list1[:], offs)
        nc.sync.dma_start(list3[:], offs3)
        load_tb(0)
        load_plane_rows(xt_plane, xt_scales, 0, range(PACK))
        load_row_values(st_cols, st)
        load_row_values(sa_cols, sa)
        load_tb(1)
        nc.sync.dma_start(list5[:], offs5)
        nc.sync.dma_start(list4[:], offs4)
        load_tb(2)
        load_plane_rows(last_plane, ws_scales, N, range(PACK - 1))
        load_tb(3)
        load_fp8_words(ws_w, ws_words)
        load_plane_rows(last_plane, ws_scales, N, range(PACK - 1, PACK))
        load_fp8_words(wb_w, wb_words)
        load_plane_rows(last_plane, wb_scales, 0, range(PACK))

        for q in range(QUADS):
            live = slice(QUAD * q, QUAD * q + PACK)
            staged = slice(HALF * (q // 2), HALF * (q // 2) + PACK)
            nc.vector.tensor_copy(first_plane[live, :].bitcast(I32), first_stage[staged, q % 2, :])
            nc.vector.tensor_copy(xo_plane[live, :].bitcast(I32), xo_stage[staged, q % 2, :])

        xt1_w = tile("xt1_w", [P, J], U32)
        xt1_plane = tile("xt1_plane", [P, J], U8)
        xo2_w = tile("xo2_w", [P, J], U16)
        xo2_plane = tile("xo2_plane", [P, J], U8)
        dealt_plane = tile("dealt_plane", [P, 2 * R], U8)
        w_dealt = tile("w_dealt", [P, R], U16)
        w0_dealt = tile("w0_dealt", [P, R], U32)

        nc.vector.tensor_copy(
            dealt_plane[:].rearrange("p (g t c i) -> p g c t i", g=2, t=PACK, i=LINE),
            first_plane[:].rearrange("p (g c i t) -> p g c t i", g=2, t=PACK, i=LINE),
        )
        nc.vector.tensor_copy(xo2_w[:], xo_w[:].indirect(list2[:]))
        nc.vector.tensor_copy(xo2_plane[:], xo_plane[:].indirect(list2[:]))
        nc.vector.tensor_copy(xt1_w[:], xt_w[:].indirect(list1[:]))
        nc.vector.tensor_copy(xt1_plane[:], xt_plane[:].indirect(list1[:]))
        for dealt, loaded, word_bytes in ((w0_dealt, w0_w, 4), (w_dealt, w_w, 2)):
            nc.scalar.copy(
                dealt[:].rearrange("p (t c i) -> p c t i", t=PACK, i=LINE // word_bytes),
                loaded[:].rearrange("p (c i t) -> p c t i", t=PACK, i=LINE // word_bytes),
            )

        a_ps = [ps.tile([P, J], F32, name="a_ps%d" % t) for t in range(PACK)]
        for t in range(PACK):
            nc.tensor.matmul_mx(
                out=a_ps[t][:], lhsT=w0_dealt[:, P * t : P * (t + 1)].bitcast(E5M2),
                lhsT_scale=dealt_plane[:, R + P * t : R + P * (t + 1)],
                rhs=xo2_w[:].bitcast(E2M1), rhs_scale=xo2_plane[:], start=True, stop=False,
            )
        for t in range(PACK):
            nc.tensor.matmul_mx(
                out=a_ps[t][:], lhsT=w_dealt[:, P * t : P * (t + 1)].bitcast(E2M1),
                lhsT_scale=dealt_plane[:, P * t : P * (t + 1)],
                rhs=xt1_w[:].bitcast(E4M3), rhs_scale=xt1_plane[:], start=False, stop=True,
            )

        xt5_w = tile("xt5_w", [P, O], U32)
        xt5_plane = tile("xt5_plane", [P, O], U8)
        nc.vector.tensor_copy(xt5_w[:], xt_w[:].indirect(list5[:]))
        nc.vector.tensor_copy(xt5_plane[:], xt_plane[:].indirect(list5[:]))
        y_ps = [ps.tile([P, O], F32, name="y_ps%d" % h) for h in range(N // P)]
        for h in range(N // P):
            nc.tensor.matmul_mx(
                out=y_ps[h][:], lhsT=ws_w[:, P * h : P * (h + 1)].bitcast(E5M2),
                lhsT_scale=last_plane[:, N + P * h : N + P * (h + 1)],
                rhs=xt5_w[:].bitcast(E4M3), rhs_scale=xt5_plane[:], start=True, stop=False,
            )

        level = tile("level", [P, PACK, O], F32)
        diff = tile("diff", [P, PACK, O], F32)

        def fetch_level(t):
            nc.scalar.activation(
                out=level[:, t, :], in_=tb_slices[t][:].indirect(list3[:]), func=ACT.Copy, scale=st_cols[:, t : t + 1]
            )

        def fetch_weighted(t, dst):
            a_sb = tile("a_sb%d" % t, [P, J], F32)
            nc.vector.tensor_copy(a_sb[:], a_ps[t][:])
            nc.scalar.activation(out=dst, in_=a_sb[:].indirect(list4[:]), func=ACT.Copy, scale=sa_cols[:, t : t + 1])

        fetch_level(0)
        fetch_level(1)
        weighted_low = tile("weighted_low", [P, 2, O], F32, "tb1")
        weighted_high = tile("weighted_high", [P, 2, O], F32)
        for t in range(PACK):
            fetch_weighted(t, (weighted_low, weighted_high)[t // 2][:, t % 2, :])
        fetch_level(2)
        fetch_level(3)

        hid = tile("hid", [P, O * PACK], BF16)
        hid_w = tile("hid_w", [P, O], U32)
        hid_plane = tile("hid_plane", [P, O], U8)
        hid_ot = hid[:].rearrange("p (o t) -> p o t", t=PACK)
        diff_ot = diff[:].rearrange("p t o -> p o t")
        nc.vector.tensor_tensor(diff[:, 0:2, :], level[:, 0:2, :], weighted_low[:], ALU.subtract)
        nc.vector.scalar_tensor_tensor(
            hid_ot[:, :, 0:2], diff_ot[:, :, 0:2], -1.0, diff_ot[:, :, 0:2], ALU.mult, ALU.max
        )
        for t in range(2, PACK):
            nc.vector.tensor_tensor(diff[:, t, :], level[:, t, :], weighted_high[:, t - 2, :], ALU.subtract)
        nc.scalar.activation(out=hid_ot[:, :, 2:4], in_=diff_ot[:, :, 2:4], func=ACT.Abs)
        nc.vector.quantize_mx(out=hid_w[:].bitcast(E4M3), scales=hid_plane[:], in_=hid[:])

        y_sb = tile("y_sb", [P, N // P, O], F32)
        for h in range(N // P):
            nc.tensor.matmul_mx(
                out=y_ps[h][:], lhsT=wb_w[:, P * h : P * (h + 1)].bitcast(E5M2),
                lhsT_scale=last_plane[:, P * h : P * (h + 1)],
                rhs=hid_w[:].bitcast(E4M3), rhs_scale=hid_plane[:], start=False, stop=True,
            )
        nc.vector.tensor_copy(y_sb[:, 0, :], y_ps[0][:])
        nc.scalar.copy(y_sb[:, 1, :], y_ps[1][:])
        nc.sync.dma_start(out.rearrange("(h p) o -> p h o", p=P), y_sb[:])
